import numpy as np
import ml_dtypes


def mxq(x, axis, fmt="e4m3"):
    dtype, down = {"e4m3": (ml_dtypes.float8_e4m3fn, 7), "e5m2": (ml_dtypes.float8_e5m2, 14)}[fmt]
    v = np.moveaxis(np.asarray(x, np.float32).astype(ml_dtypes.bfloat16).astype(np.float64), axis, -1)
    blocks = v.reshape(v.shape[:-1] + (-1, 32))
    amax = np.abs(blocks).max(-1, keepdims=True)
    byte = np.maximum(np.where(amax > 0, np.frexp(amax)[1] - 1 + 127, 0) - down, 1)
    scale = np.exp2(byte - 127.0)
    codes = (blocks / scale).astype(np.float32).astype(dtype).astype(np.float64)
    return np.moveaxis((codes * scale).reshape(v.shape), -1, axis)


WIDE = False


def mx_kscale(k):
    if not WIDE:
        return np.ones(k)
    levels = np.array([10, -10, 5, -5, 0])
    if k % 512:
        return np.exp2(np.random.permutation(np.resize(levels, k // 32))).repeat(32)
    a = np.empty((k // 512, 16))
    for p in range(k // 512):
        a[p, :8] = np.random.permutation(np.resize(levels, 8))
        for g in range(8):
            far = levels[np.abs(levels - a[p, g]) >= 10]
            a[p, g + 8] = far[np.random.randint(len(far))]
    return np.exp2(a.ravel()).repeat(32)


def f64(x):
    return np.asarray(x).astype(np.float64)


def striped(idx):
    return np.tile(np.asarray(idx).reshape(-1, 16).T, (8, 1)).astype(np.uint16)


def unstriped(offs):
    return offs[:16].T.reshape(-1).astype(np.int64)


E2M1 = np.array([0.0, 0.5, 1.0, 1.5, 2.0, 3.0, 4.0, 6.0, -0.0, -0.5, -1.0, -1.5, -2.0, -3.0, -4.0, -6.0])


def pack_weight(w, fmt):
    k, n = w.shape
    w = f64(np.asarray(w, np.float32).astype(ml_dtypes.bfloat16)).reshape(k // 32, 32, n)
    amax = np.abs(w).max(1)
    if fmt == "e4m3":
        byte = np.frexp(amax)[1] - 1 + 127 - 7
    else:
        mant, ex = np.frexp(amax / 6.0)
        byte = np.where(mant > 0.5, ex, ex - 1) + 127
    byte = np.clip(np.where(amax > 0, byte, 1), 1, 254)
    scaled = (w * np.exp2(127.0 - byte)[:, None, :]).reshape(k, n).astype(np.float32)
    by_word = np.ascontiguousarray(scaled.reshape(k // 512, 128, 4, n).transpose(0, 1, 3, 2))
    if fmt == "e4m3":
        words = by_word.astype(ml_dtypes.float8_e4m3fn).view(np.uint8)
    else:
        c = by_word.astype(ml_dtypes.float4_e2m1fn).view(np.uint8) & 0xF
        words = (c[..., 0::2] | (c[..., 1::2] << 4)).reshape(k // 512, 128, 2 * n)
    return np.ascontiguousarray(words), np.ascontiguousarray(byte.astype(np.uint8).reshape(k // 512, 16, n))


def unpack_weight(words, scales, fmt):
    g, _, n = scales.shape
    words = np.ascontiguousarray(words).reshape(g, 128, n, -1)
    if fmt == "e4m3":
        vals = words.view(ml_dtypes.float8_e4m3fn).astype(np.float64)
    else:
        nib = np.empty((g, 128, n, 4), np.uint8)
        nib[..., 0::2] = words & 0xF
        nib[..., 1::2] = words >> 4
        vals = E2M1[nib]
    vals = vals * np.repeat(np.exp2(scales.astype(np.float64) - 127.0), 8, axis=1)[..., None]
    return vals.transpose(0, 1, 3, 2).reshape(g * 512, n)


def bf(x):
    return np.asarray(x, np.float32).astype(ml_dtypes.bfloat16)


def planes(Y):
    r, m = Y.shape
    b = f64(bf(Y)).reshape(r // 32, 32, m)
    amax = np.abs(b).max(1)
    byte = np.clip(np.where(amax > 0, np.frexp(amax)[1] - 1 + 127 - 7, 1), 1, 254)
    codes = (b * np.exp2(127.0 - byte)[:, None, :]).reshape(r, m).astype(np.float32).astype(ml_dtypes.float8_e4m3fn).view(np.uint8)
    words = codes.reshape(r // 512, 128, 4, m).transpose(0, 1, 3, 2)
    return np.ascontiguousarray(words), np.ascontiguousarray(byte.astype(np.uint8).reshape(r // 512, 16, m))


D, T, I, J, U, Z, E, Y = 512, 2048, 512, 512, 1024, 1024, 512, 1024


def setup_inputs():
    n = np.random.standard_normal
    idx = np.random.permutation(T)[:I]
    idx2 = np.random.permutation(U)[:J]
    idx3 = np.random.permutation(Z)[:J]
    idx4 = np.random.permutation(Y)[:I]
    fd = mx_kscale(D)
    fi = mx_kscale(I)
    ti = np.ones(T)
    ti[idx] = fi
    ti4 = np.ones(Y)
    ti4[idx4] = fi
    keysp = pack_weight(n((D, T)) / fd[:, None], "e2m1")
    return {
        "keys_words": keysp[0],
        "keys_scales": keysp[1],
        "notes": (n((D, U)) * 1.0 / np.sqrt(D) * fd[:, None]).astype(np.float32),
        "users2": (n((D, Z)) * 1.0 / np.sqrt(D) * fd[:, None]).astype(np.float32),
        "rowf": (np.random.uniform(0.02, 0.08, (I, 1)) * fi[:, None]).astype(np.float32),
        "rowf2": (np.random.uniform(0.02, 0.08, (I, 1)) * fi[:, None]).astype(np.float32),
        "vals": (n((E, T)) / ti).astype(np.float32),
        "vals2": (n((E, Y)) / ti4).astype(np.float32),
        "offs": striped(idx),
        "offs2": striped(idx2),
        "offs3": striped(idx3),
        "offs4": striped(idx4),
    }


def reference(keys_words, keys_scales, notes, users2, rowf, rowf2, vals, vals2, offs, offs2, offs3, offs4):
    idx = unstriped(offs)
    idx2 = unstriped(offs2)
    idx3 = unstriped(offs3)
    idx4 = unstriped(offs4)
    keysu = unpack_weight(keys_words, keys_scales, "e2m1")
    keysidxg = keysu[:, idx]
    notesidx2q = mxq(f64(notes)[:, idx2], 0, "e4m3")
    g1 = keysidxg.T @ notesidx2q
    users2idx3q = mxq(f64(users2)[:, idx3], 0, "e4m3")
    g2 = keysidxg.T @ users2idx3q
    g0 = np.maximum(g1, g2)
    gr1 = g0 * f64(rowf)
    gr2 = g0 * f64(rowf2)
    vt1 = f64(vals)[:, idx].T
    vt2 = f64(vals2)[:, idx4].T
    vt1q = mxq(vt1, 0, "e4m3")
    gr1q = mxq(gr1, 0, "e4m3")
    vt2q = mxq(vt2, 0, "e4m3")
    gr2q = mxq(gr2, 0, "e4m3")
    o = vt1q.T @ gr1q + vt2q.T @ gr2q
    words, scales = planes(o)
    return o, words, scales

@@ -1,0 +1,262 @@
+from contextlib import ExitStack
+
+import concourse.mybir as mybir
+from concourse.masks import make_identity
+
+F32 = mybir.dt.float32
+BF16 = mybir.dt.bfloat16
+I32 = mybir.dt.int32
+U32 = mybir.dt.uint32
+U16 = mybir.dt.uint16
+U8 = mybir.dt.uint8
+FP8X4 = mybir.dt.float8_e4m3fn_x4
+FP4X4 = mybir.dt.float4_e2m1fn_x4
+COPY = mybir.ActivationFunctionType.Copy
+MAX = mybir.AluOpType.max
+MULT = mybir.AluOpType.mult
+
+P = 128
+PACK = 4
+N = 512
+BLK = 128
+NBLK = N // BLK
+HALF = N // 2
+LIST_COLS = N // 16
+
+FLOPS = 4 * 2 * 512 * 512 * 512
+
+
+def tile_attend_tab_larger_twostores_pl_kernel(
+    tc, keys_words, keys_scales, notes, users2, rowf, rowf2, vals, vals2, offs, offs2, offs3, offs4, out_0, out_1, out_2
+):
+    nc = tc.nc
+    tokens = keys_scales.shape[2]
+
+    with ExitStack() as ctx:
+        held = ctx.enter_context(tc.tile_pool(name="held", bufs=1))
+        table_psum = ctx.enter_context(tc.psum_pool(name="table_psum", bufs=NBLK))
+        turn_psum = ctx.enter_context(tc.psum_pool(name="turn_psum", bufs=4))
+
+        def load_list(name, src):
+            lst = held.tile([P, LIST_COLS], U16, name=name)
+            nc.sync.dma_start(lst[:], src)
+            return lst
+
+        def load_plane(name, pool, t):
+            plane = held.tile([P, pool.shape[1]], F32, name="%s%d" % (name, t), tag="%s%d" % (name, t), align_bytes=64)
+            nc.sync.dma_start(plane[:], pool.rearrange("(p t) c -> t p c", t=PACK)[t])
+            return plane
+
+        def gather(engine, dst, plane, lst):
+            if engine == "V":
+                nc.vector.tensor_copy(dst, plane[:].indirect(lst))
+            else:
+                nc.scalar.activation(dst, plane[:].indirect(lst), COPY)
+
+        def gather_split(dst, plane, lst):
+            gather("V", dst[:, :HALF], plane, lst[:, : LIST_COLS // 2])
+            gather("S", dst[:, HALF:], plane, lst[:, LIST_COLS // 2 :])
+
+        def copy(engine, dst, src):
+            if engine == "V":
+                nc.vector.tensor_copy(dst, src)
+            else:
+                nc.scalar.copy(dst, src)
+
+        def mx_tiles(name, width):
+            codes = held.tile([P, width], U32, name=name + "_codes", align_bytes=64)
+            scales = held.tile([P, width], U8, name=name + "_scales", align_bytes=64)
+            return codes, scales
+
+        def quantise(mx, cols, woven):
+            nc.vector.quantize_mx(out=mx[0][:, cols].bitcast(FP8X4), scales=mx[1][:, cols], in_=woven)
+
+        list2 = load_list("list2", offs2)
+        note_planes = [load_plane("notes", notes, 0)]
+        key_bytes = held.tile([P, tokens], U8, name="key_bytes")
+        nc.vector.memset(key_bytes[:].bitcast(I32), 0)
+        for q in range(4):
+            nc.scalar.dma_start(
+                key_bytes[32 * q : 32 * q + 4, :].bitcast(I32), keys_scales[0, 4 * q : 4 * q + 4, :].bitcast(I32)
+            )
+        list1 = load_list("list1", offs)
+        note_planes.extend(load_plane("notes", notes, t) for t in range(1, PACK))
+        key_words = held.tile([P, tokens], U16, name="key_words")
+        nc.sync.dma_start(key_words[:].bitcast(I32), keys_words[0].bitcast(I32))
+        user_planes = [load_plane("users", users2, 0)]
+        list3 = load_list("list3", offs3)
+        user_planes.extend(load_plane("users", users2, t) for t in range(1, PACK))
+        list4 = load_list("list4", offs4)
+        factors = held.tile([P, 2, 2 * PACK], F32, name="factors")
+        for k, src in enumerate((rowf, rowf2)):
+            nc.sync.dma_start(factors[:, k, :PACK], src.rearrange("(p r) o -> p (r o)", r=PACK))
+        val2_planes = [load_plane("vals2_", vals2, t) for t in range(PACK)]
+        val1_planes = [load_plane("vals1_", vals, t) for t in range(PACK)]
+        identity = held.tile([P, P], F32, name="identity")
+        make_identity(nc, identity[:])
+
+        dealt_words = held.tile([P, PACK, BLK], U16, name="dealt_words", align_bytes=64)
+        dealt_bytes = held.tile([P, PACK, BLK], U8, name="dealt_bytes", align_bytes=64)
+        nc.vector.tensor_copy(dealt_bytes[:].rearrange("p r s -> p s r"), key_bytes[:].indirect(list1[:]))
+
+        def weave(engine, woven, picked, cols):
+            copy(
+                engine,
+                woven[:, cols, :].rearrange("p (c i) t -> p c t i", i=4),
+                picked[:, :, cols].rearrange("p t (c i) -> p c t i", i=4),
+            )
+
+        def table_products(mx, jb):
+            bank = table_psum.tile([P, PACK, BLK], F32, name="table_bank")
+            cols = slice(jb * BLK, (jb + 1) * BLK)
+            for r in range(PACK):
+                nc.tensor.matmul_mx(
+                    out=bank[:, r, :],
+                    lhsT=dealt_words[:, r, :].bitcast(FP4X4),
+                    lhsT_scale=dealt_bytes[:, r, :],
+                    rhs=mx[0][:, cols].bitcast(FP8X4),
+                    rhs_scale=mx[1][:, cols],
+                    start=True,
+                    stop=True,
+                )
+            return bank
+
+        halves = [slice(0, HALF), slice(HALF, N)]
+
+        last = PACK - 1
+
+        picked_notes = held.tile([P, PACK, N], BF16, name="picked_notes")
+        for t in range(last):
+            gather("S", picked_notes[:, t, :], note_planes[t], list2[:])
+        gather_split(picked_notes[:, last, :], note_planes[last], list2)
+        woven_notes = held.tile([P, N, PACK], BF16, name="woven_notes", align_bytes=64)
+        notes_mx = mx_tiles("notes", N)
+        weave("V", woven_notes, picked_notes, halves[0])
+        weave("S", woven_notes, picked_notes, halves[1])
+        picked_words = held.tile([P, N], U16, name="picked_words")
+        nc.vector.tensor_copy(picked_words[:], key_words[:].indirect(list1[:]))
+        nc.vector.tensor_copy(dealt_words[:], picked_words[:].rearrange("p (s r) -> p r s", r=PACK))
+        for cols in halves:
+            quantise(notes_mx, cols, woven_notes[:, cols, :].rearrange("p c t -> p (c t)"))
+        picked_users = held.tile([P, PACK, N], BF16, name="picked_users")
+        gather("S", picked_users[:, 0, :], user_planes[0], list3[:])
+        gather_split(picked_users[:, 1, :], user_planes[1], list3)
+        gather("V", picked_users[:, 2, :], user_planes[2], list3[:])
+        gather_split(picked_users[:, last, :], user_planes[last], list3)
+        g1_first = held.tile([P, 2, BLK, PACK], F32, name="g1_first")
+        g1_rest = held.tile([P, 2, BLK, PACK], F32, name="g1_rest", tag="users%d" % last, align_bytes=64)
+        g1 = [g1_first[:, 0], g1_first[:, 1], g1_rest[:, 0], g1_rest[:, 1]]
+        for jb in range(NBLK):
+            bank = table_products(notes_mx, jb)
+            nc.scalar.copy(g1[jb], bank[:].rearrange("p r j -> p j r"))
+
+        woven_users = held.tile([P, N, PACK], BF16, name="woven_users", tag="woven_users", align_bytes=64)
+        users_mx = mx_tiles("users", N)
+        for cols in halves:
+            weave("V", woven_users, picked_users, cols)
+        for cols in halves:
+            quantise(users_mx, cols, woven_users[:, cols, :].rearrange("p c t -> p (c t)"))
+
+        g0 = []
+        for jb in range(NBLK):
+            bank = table_products(users_mx, jb)
+            larger = held.tile([P, 1, BLK, PACK], F32, name="g0_%d" % jb, tag="g0_%d" % jb, align_bytes=64)
+            nc.vector.tensor_tensor(larger[:, 0], bank[:].rearrange("p r j -> p j r"), g1[jb], MAX)
+            g0.append(larger)
+        gr = held.tile([P, NBLK, 2, BLK, PACK], BF16, name="gr", align_bytes=64)
+        gr_mx = mx_tiles("gr", 2 * N)
+        spread = factors[:, :, :PACK].rearrange("p k (o r) -> p k o r", o=1).to_broadcast([P, 2, BLK, PACK])
+
+        def weigh(jb):
+            nc.vector.tensor_tensor(gr[:, jb], g0[jb][:].to_broadcast([P, 2, BLK, PACK]), spread, MULT)
+            quantise(gr_mx, slice(2 * jb * BLK, 2 * (jb + 1) * BLK), gr[:, jb].rearrange("p k c t -> p (k c t)"))
+
+        def pick_values(name, plane, lst, split, tag):
+            picked = held.tile([P, N], BF16, name=name + "_picked", tag=tag, align_bytes=64)
+            if split:
+                gather_split(picked[:], plane, lst)
+            else:
+                gather("S", picked[:], plane, lst[:])
+            return picked
+
+        def turn(group):
+            turned = turn_psum.tile([P, len(group), 2, BLK], F32, name="turned")
+            for n, picked in enumerate(group):
+                words = picked[:].bitcast(F32)
+                for u in range(2):
+                    nc.tensor.transpose(turned[:, n, u, :], words[:, u : HALF : 2], identity[:])
+            return turned
+
+        def weave_turned(engine, name, turned, count, tag):
+            woven = held.tile([P, count * BLK * PACK], BF16, name=name + "_woven", tag=tag, align_bytes=64)
+            copy(
+                engine,
+                woven[:].bitcast(F32).rearrange("p (n e u) -> p n e u", n=count, u=2),
+                turned[:].rearrange("p n u e -> p n e u"),
+            )
+            mx = mx_tiles(name, count * BLK)
+            quantise(mx, slice(0, count * BLK), woven[:])
+            return mx
+
+        out_banks = [table_psum.tile([P, PACK, BLK], F32, name="table_bank") for jb in range(NBLK)]
+
+        def out_pass(t, jb, vt, n, k, start, stop):
+            cols = slice((2 * jb + k) * BLK, (2 * jb + k + 1) * BLK)
+            rows = slice(n * BLK, (n + 1) * BLK)
+            nc.tensor.matmul_mx(
+                out=out_banks[jb][:, t, :],
+                lhsT=vt[0][:, rows].bitcast(FP8X4),
+                lhsT_scale=vt[1][:, rows],
+                rhs=gr_mx[0][:, cols].bitcast(FP8X4),
+                rhs_scale=gr_mx[1][:, cols],
+                start=start,
+                stop=stop,
+            )
+
+        picked2 = [
+            pick_values("vt2_0", val2_planes[0], list4, False, "vt2_0_picked"),
+            pick_values("vt2_1", val2_planes[1], list4, False, "woven_users"),
+        ]
+        turned = turn(picked2)
+        weigh(0)
+        val2_mx = [weave_turned("V", "vt2_a", turned, 2, "g0_0")]
+        picked2 = [pick_values("vt2_%d" % t, val2_planes[t], list4, False, "vt2_%d_picked" % t) for t in range(2, PACK)]
+        turned = turn(picked2)
+        picked1 = pick_values("vt1_0", val1_planes[0], list1, False, "vt1_0_picked")
+        weigh(1)
+        weigh(2)
+        val2_mx.append(weave_turned("S", "vt2_b", turned, 2, "vals1_0"))
+        weigh(3)
+        for jb in range(NBLK):
+            for t in range(PACK):
+                out_pass(t, jb, val2_mx[t // 2], t % 2, 1, t == 0, False)
+        for t in range(PACK):
+            turned = turn([picked1])
+            tag = "vt1_last_woven"
+            if t < last:
+                picked1 = pick_values("vt1_%d" % (t + 1), val1_planes[t + 1], list1, t + 1 == last, "vt1_%d_picked" % (t + 1))
+                tag = "vals1_%d" % (t + 1)
+            mx = weave_turned("S", "vt1_%d" % t, turned, 1, tag)
+            for jb in range(NBLK):
+                out_pass(t, jb, mx, 0, 0, False, t == last)
+
+        result = held.tile([P, NBLK, PACK, BLK], F32, name="result")
+        out_rows = out_0.rearrange("(p t) (b j) -> b p t j", t=PACK, j=BLK)
+        woven_out = held.tile([P, N, PACK], BF16, name="woven_out", align_bytes=64)
+        out_mx = mx_tiles("out", N)
+        for jb in range(NBLK):
+            cols = slice(jb * BLK, (jb + 1) * BLK)
+            copy("VSVS"[jb], woven_out[:, cols, :], out_banks[jb][:].rearrange("p t j -> p j t"))
+        for jb in range(NBLK):
+            cols = slice(jb * BLK, (jb + 1) * BLK)
+            quantise(out_mx, cols, woven_out[:, cols, :].rearrange("p c t -> p (c t)"))
+        out_words = out_1[0].rearrange("p c r -> p (c r)").bitcast(I32)
+        for cols in halves:
+            nc.sync.dma_start(out_words[:, cols], out_mx[0][:, cols].bitcast(I32))
+        for q in range(4):
+            nc.sync.dma_start(
+                out_2[0, 4 * q : 4 * q + 4, :].bitcast(I32), out_mx[1][32 * q : 32 * q + 4, :].bitcast(I32)
+            )
+        for jb in range(NBLK):
+            copy("SSSV"[jb], result[:, jb], out_banks[jb][:])
+            nc.sync.dma_start(out_rows[jb], result[:, jb])

@@ -35,7 +35,8 @@ def tile_attend_tab_larger_twostores_pl_kernel(
     with ExitStack() as ctx:
         held = ctx.enter_context(tc.tile_pool(name="held", bufs=1))
         table_psum = ctx.enter_context(tc.psum_pool(name="table_psum", bufs=NBLK))
-        turn_psum = ctx.enter_context(tc.psum_pool(name="turn_psum", bufs=4))
+        turn_psum = ctx.enter_context(tc.psum_pool(name="turn_psum", bufs=3))
+        last_psum = ctx.enter_context(tc.psum_pool(name="last_psum", bufs=1))
 
         def load_list(name, src):
             lst = held.tile([P, LIST_COLS], U16, name=name)
@@ -63,8 +64,8 @@ def tile_attend_tab_larger_twostores_pl_kernel(
             else:
                 nc.scalar.copy(dst, src)
 
-        def mx_tiles(name, width):
-            codes = held.tile([P, width], U32, name=name + "_codes", align_bytes=64)
+        def mx_tiles(name, width, tag=None):
+            codes = held.tile([P, width], U32, name=name + "_codes", tag=tag or name + "_codes", align_bytes=64)
             scales = held.tile([P, width], U8, name=name + "_scales", align_bytes=64)
             return codes, scales
 
@@ -73,16 +74,16 @@ def tile_attend_tab_larger_twostores_pl_kernel(
 
         list2 = load_list("list2", offs2)
         note_planes = [load_plane("notes", notes, 0)]
+        key_words = held.tile([P, tokens], U16, name="key_words")
+        nc.sync.dma_start(key_words[:].bitcast(I32), keys_words[0].bitcast(I32))
         key_bytes = held.tile([P, tokens], U8, name="key_bytes")
-        nc.vector.memset(key_bytes[:].bitcast(I32), 0)
+        nc.gpsimd.memset(key_bytes[:].bitcast(I32), 0)
         for q in range(4):
             nc.scalar.dma_start(
                 key_bytes[32 * q : 32 * q + 4, :].bitcast(I32), keys_scales[0, 4 * q : 4 * q + 4, :].bitcast(I32)
             )
         list1 = load_list("list1", offs)
         note_planes.extend(load_plane("notes", notes, t) for t in range(1, PACK))
-        key_words = held.tile([P, tokens], U16, name="key_words")
-        nc.sync.dma_start(key_words[:].bitcast(I32), keys_words[0].bitcast(I32))
         user_planes = [load_plane("users", users2, 0)]
         list3 = load_list("list3", offs3)
         user_planes.extend(load_plane("users", users2, t) for t in range(1, PACK))
@@ -95,7 +96,10 @@ def tile_attend_tab_larger_twostores_pl_kernel(
         identity = held.tile([P, P], F32, name="identity")
         make_identity(nc, identity[:])
 
+        picked_words = held.tile([P, N], U16, name="picked_words")
+        nc.vector.tensor_copy(picked_words[:], key_words[:].indirect(list1[:]))
         dealt_words = held.tile([P, PACK, BLK], U16, name="dealt_words", align_bytes=64)
+        nc.vector.tensor_copy(dealt_words[:], picked_words[:].rearrange("p (s r) -> p r s", r=PACK))
         dealt_bytes = held.tile([P, PACK, BLK], U8, name="dealt_bytes", align_bytes=64)
         nc.vector.tensor_copy(dealt_bytes[:].rearrange("p r s -> p s r"), key_bytes[:].indirect(list1[:]))
 
@@ -131,24 +135,21 @@ def tile_attend_tab_larger_twostores_pl_kernel(
         gather_split(picked_notes[:, last, :], note_planes[last], list2)
         woven_notes = held.tile([P, N, PACK], BF16, name="woven_notes", align_bytes=64)
         notes_mx = mx_tiles("notes", N)
-        weave("V", woven_notes, picked_notes, halves[0])
-        weave("S", woven_notes, picked_notes, halves[1])
-        picked_words = held.tile([P, N], U16, name="picked_words")
-        nc.vector.tensor_copy(picked_words[:], key_words[:].indirect(list1[:]))
-        nc.vector.tensor_copy(dealt_words[:], picked_words[:].rearrange("p (s r) -> p r s", r=PACK))
+        for cols in halves:
+            weave("V", woven_notes, picked_notes, cols)
         for cols in halves:
             quantise(notes_mx, cols, woven_notes[:, cols, :].rearrange("p c t -> p (c t)"))
-        picked_users = held.tile([P, PACK, N], BF16, name="picked_users")
-        gather("S", picked_users[:, 0, :], user_planes[0], list3[:])
-        gather_split(picked_users[:, 1, :], user_planes[1], list3)
-        gather("V", picked_users[:, 2, :], user_planes[2], list3[:])
+        picked_users = held.tile([P, PACK, N], BF16, name="picked_users", tag="picked_users", align_bytes=64)
+        for t in range(last):
+            gather("SSV"[t], picked_users[:, t, :], user_planes[t], list3[:])
         gather_split(picked_users[:, last, :], user_planes[last], list3)
-        g1_first = held.tile([P, 2, BLK, PACK], F32, name="g1_first")
-        g1_rest = held.tile([P, 2, BLK, PACK], F32, name="g1_rest", tag="users%d" % last, align_bytes=64)
-        g1 = [g1_first[:, 0], g1_first[:, 1], g1_rest[:, 0], g1_rest[:, 1]]
+        g1_first = held.tile([P, 1, BLK, PACK], F32, name="g1_first", tag="users1", align_bytes=64)
+        g1_rest = held.tile([P, NBLK - 2, BLK, PACK], F32, name="g1_rest", tag="users%d" % last, align_bytes=64)
+        g1 = [g1_first[:, 0]] + [g1_rest[:, n] for n in range(NBLK - 2)]
         for jb in range(NBLK):
             bank = table_products(notes_mx, jb)
-            nc.scalar.copy(g1[jb], bank[:].rearrange("p r j -> p j r"))
+            if jb < NBLK - 1:
+                nc.scalar.copy(g1[jb], bank[:].rearrange("p r j -> p j r"))
 
         woven_users = held.tile([P, N, PACK], BF16, name="woven_users", tag="woven_users", align_bytes=64)
         users_mx = mx_tiles("users", N)
@@ -157,26 +158,33 @@ def tile_attend_tab_larger_twostores_pl_kernel(
         for cols in halves:
             quantise(users_mx, cols, woven_users[:, cols, :].rearrange("p c t -> p (c t)"))
 
-        g0 = []
+        g1_last = held.tile([P, BLK, PACK], F32, name="g1_last", tag="woven_users", align_bytes=64)
+        nc.vector.tensor_copy(g1_last[:], bank[:].rearrange("p r j -> p j r"))
+        g1.append(g1_last[:])
+
+        g0 = [held.tile([P, 1, HALF, PACK], F32, name="g0_%d" % h, tag="g0_%d" % h, align_bytes=64) for h in range(2)]
         for jb in range(NBLK):
             bank = table_products(users_mx, jb)
-            larger = held.tile([P, 1, BLK, PACK], F32, name="g0_%d" % jb, tag="g0_%d" % jb, align_bytes=64)
-            nc.vector.tensor_tensor(larger[:, 0], bank[:].rearrange("p r j -> p j r"), g1[jb], MAX)
-            g0.append(larger)
-        gr = held.tile([P, NBLK, 2, BLK, PACK], BF16, name="gr", align_bytes=64)
-        gr_mx = mx_tiles("gr", 2 * N)
-        spread = factors[:, :, :PACK].rearrange("p k (o r) -> p k o r", o=1).to_broadcast([P, 2, BLK, PACK])
+            cols = slice((jb % 2) * BLK, (jb % 2 + 1) * BLK)
+            nc.vector.tensor_tensor(g0[jb // 2][:, 0, cols], bank[:].rearrange("p r j -> p j r"), g1[jb], MAX)
+        gr = []
+        gr_mx = []
+        spread = factors[:, :, :PACK].rearrange("p k (o r) -> p k o r", o=1).to_broadcast([P, 2, HALF, PACK])
 
-        def weigh(jb):
-            nc.vector.tensor_tensor(gr[:, jb], g0[jb][:].to_broadcast([P, 2, BLK, PACK]), spread, MULT)
-            quantise(gr_mx, slice(2 * jb * BLK, 2 * (jb + 1) * BLK), gr[:, jb].rearrange("p k c t -> p (k c t)"))
+        def weigh(h, tag):
+            gr.append(held.tile([P, 2, HALF, PACK], BF16, name="gr_%d" % h, tag=tag, align_bytes=64))
+            nc.vector.tensor_tensor(gr[h][:], g0[h][:].to_broadcast([P, 2, HALF, PACK]), spread, MULT)
 
-        def pick_values(name, plane, lst, split, tag):
+        def quantise_weights(h, tag):
+            gr_mx.append(mx_tiles("gr%d" % h, N, tag))
+            quantise(gr_mx[h], slice(0, N), gr[h][:].rearrange("p k c t -> p (k c t)"))
+
+        def pick_values(name, plane, lst, engine, tag):
             picked = held.tile([P, N], BF16, name=name + "_picked", tag=tag, align_bytes=64)
-            if split:
+            if engine == "B":
                 gather_split(picked[:], plane, lst)
             else:
-                gather("S", picked[:], plane, lst[:])
+                gather(engine, picked[:], plane, lst[:])
             return picked
 
         def turn(group):
@@ -187,76 +195,83 @@ def tile_attend_tab_larger_twostores_pl_kernel(
                     nc.tensor.transpose(turned[:, n, u, :], words[:, u : HALF : 2], identity[:])
             return turned
 
-        def weave_turned(engine, name, turned, count, tag):
+        def weave_turned(engine, name, turned, count, tag, mx=None, first=0):
             woven = held.tile([P, count * BLK * PACK], BF16, name=name + "_woven", tag=tag, align_bytes=64)
             copy(
                 engine,
                 woven[:].bitcast(F32).rearrange("p (n e u) -> p n e u", n=count, u=2),
                 turned[:].rearrange("p n u e -> p n e u"),
             )
-            mx = mx_tiles(name, count * BLK)
-            quantise(mx, slice(0, count * BLK), woven[:])
+            mx = mx or mx_tiles(name, count * BLK)
+            quantise(mx, slice(first * BLK, (first + count) * BLK), woven[:])
             return mx
 
-        out_banks = [table_psum.tile([P, PACK, BLK], F32, name="table_bank") for jb in range(NBLK)]
+        out_banks = [table_psum.tile([P, 2, HALF], F32, name="table_bank") for t in range(last)]
+        last_banks = [table_psum.tile([P, HALF], F32, name="table_bank"), last_psum.tile([P, HALF], F32, name="last_bank")]
 
-        def out_pass(t, jb, vt, n, k, start, stop):
-            cols = slice((2 * jb + k) * BLK, (2 * jb + k + 1) * BLK)
+        def out_pass(t, h, vt, n, k):
+            cols = slice(k * HALF, (k + 1) * HALF)
             rows = slice(n * BLK, (n + 1) * BLK)
             nc.tensor.matmul_mx(
-                out=out_banks[jb][:, t, :],
+                out=last_banks[h][:] if t == last else out_banks[t][:, h],
                 lhsT=vt[0][:, rows].bitcast(FP8X4),
                 lhsT_scale=vt[1][:, rows],
-                rhs=gr_mx[0][:, cols].bitcast(FP8X4),
-                rhs_scale=gr_mx[1][:, cols],
-                start=start,
-                stop=stop,
+                rhs=gr_mx[h][0][:, cols].bitcast(FP8X4),
+                rhs_scale=gr_mx[h][1][:, cols],
+                start=k == 1 and (t == last or h == 0),
+                stop=k == 0 and (t == last or h == 1),
             )
 
         picked2 = [
-            pick_values("vt2_0", val2_planes[0], list4, False, "vt2_0_picked"),
-            pick_values("vt2_1", val2_planes[1], list4, False, "woven_users"),
+            pick_values("vt2_0", val2_planes[0], list4, "S", "vt2_0_picked"),
+            pick_values("vt2_1", val2_planes[1], list4, "S", "vt2_1_picked"),
         ]
         turned = turn(picked2)
-        weigh(0)
-        val2_mx = [weave_turned("V", "vt2_a", turned, 2, "g0_0")]
-        picked2 = [pick_values("vt2_%d" % t, val2_planes[t], list4, False, "vt2_%d_picked" % t) for t in range(2, PACK)]
+        weigh(0, "gr_0")
+        quantise_weights(0, None)
+        val2_mx = [weave_turned("S", "vt2_a", turned, 2, "vals2_2")]
+        picked2 = [pick_values("vt2_%d" % t, val2_planes[t], list4, "S", "vt2_%d_picked" % t) for t in range(2, PACK)]
         turned = turn(picked2)
-        picked1 = pick_values("vt1_0", val1_planes[0], list1, False, "vt1_0_picked")
-        weigh(1)
-        weigh(2)
+        picked1 = pick_values("vt1_0", val1_planes[0], list1, "S", "vt1_0_picked")
+        weigh(1, "vals2_2")
         val2_mx.append(weave_turned("S", "vt2_b", turned, 2, "vals1_0"))
-        weigh(3)
-        for jb in range(NBLK):
-            for t in range(PACK):
-                out_pass(t, jb, val2_mx[t // 2], t % 2, 1, t == 0, False)
+        out_rows = out_0.rearrange("(p t) j -> p t j", t=PACK)
+        turned0 = turn([picked1])
+        picked1 = pick_values("vt1_1", val1_planes[1], list1, "S", "vt1_1_picked")
+        turned1 = turn([picked1])
+        quantise_weights(1, None)
+        picked1 = pick_values("vt1_2", val1_planes[2], list1, "S", "vt1_2_picked")
+        turned2 = turn([picked1])
+        picked1 = pick_values("vt1_3", val1_planes[3], list1, "V", "vt1_3_picked")
+        turned3 = turn([picked1])
+        middle_mx = mx_tiles("vt1_middle", 3 * BLK, "vals1_3")
+        val1_mx = [weave_turned("S", "vt1_0", turned0, 1, "vals1_1", middle_mx, 2)]
+        val1_mx.append(weave_turned("S", "vt1_1", turned1, 1, "vals1_2", middle_mx, 0))
+        val1_mx.append(weave_turned("S", "vt1_2", turned2, 1, "vt1_2_woven", middle_mx, 1))
+        val1_mx.append(weave_turned("S", "vt1_3", turned3, 1, "vt1_3_woven"))
+        result = held.tile([P, PACK, N], F32, name="result", tag="vt1_3_picked", align_bytes=64)
         for t in range(PACK):
-            turned = turn([picked1])
-            tag = "vt1_last_woven"
-            if t < last:
-                picked1 = pick_values("vt1_%d" % (t + 1), val1_planes[t + 1], list1, t + 1 == last, "vt1_%d_picked" % (t + 1))
-                tag = "vals1_%d" % (t + 1)
-            mx = weave_turned("S", "vt1_%d" % t, turned, 1, tag)
-            for jb in range(NBLK):
-                out_pass(t, jb, mx, 0, 0, False, t == last)
+            for h in range(2):
+                out_pass(t, h, val2_mx[t // 2], t % 2, 1)
+        for t in range(PACK):
+            for h in range(2):
+                out_pass(t, h, val1_mx[t], (2, 0, 1, 0)[t], 0)
+        for t in range(last):
+            copy("VVS"[t], result[:, t, :], out_banks[t][:].rearrange("p h j -> p (h j)"))
+        nc.sync.dma_start(out_rows[:, :last, :], result[:, :last, :])
 
-        result = held.tile([P, NBLK, PACK, BLK], F32, name="result")
-        out_rows = out_0.rearrange("(p t) (b j) -> b p t j", t=PACK, j=BLK)
         woven_out = held.tile([P, N, PACK], BF16, name="woven_out", align_bytes=64)
         out_mx = mx_tiles("out", N)
-        for jb in range(NBLK):
-            cols = slice(jb * BLK, (jb + 1) * BLK)
-            copy("VSVS"[jb], woven_out[:, cols, :], out_banks[jb][:].rearrange("p t j -> p j t"))
-        for jb in range(NBLK):
-            cols = slice(jb * BLK, (jb + 1) * BLK)
-            quantise(out_mx, cols, woven_out[:, cols, :].rearrange("p c t -> p (c t)"))
         out_words = out_1[0].rearrange("p c r -> p (c r)").bitcast(I32)
+        for h, cols in enumerate(halves):
+            nc.scalar.copy(result[:, last, cols], last_banks[h][:])
+        nc.scalar.dma_start(out_rows[:, last, :], result[:, last, :])
         for cols in halves:
+            weave("V", woven_out, result, cols)
+        for cols in halves:
+            quantise(out_mx, cols, woven_out[:, cols, :].rearrange("p c t -> p (c t)"))
             nc.sync.dma_start(out_words[:, cols], out_mx[0][:, cols].bitcast(I32))
         for q in range(4):
-            nc.sync.dma_start(
+            nc.scalar.dma_start(
                 out_2[0, 4 * q : 4 * q + 4, :].bitcast(I32), out_mx[1][32 * q : 32 * q + 4, :].bitcast(I32)
             )
-        for jb in range(NBLK):
-            copy("SSSV"[jb], result[:, jb], out_banks[jb][:])
-            nc.sync.dma_start(out_rows[jb], result[:, jb])

@@ -140,12 +140,13 @@ def tile_attend_tab_larger_twostores_pl_kernel(
         for cols in halves:
             quantise(notes_mx, cols, woven_notes[:, cols, :].rearrange("p c t -> p (c t)"))
         picked_users = held.tile([P, PACK, N], BF16, name="picked_users", tag="picked_users", align_bytes=64)
-        for t in range(last):
-            gather("SSV"[t], picked_users[:, t, :], user_planes[t], list3[:])
+        gather("S", picked_users[:, 0, :], user_planes[0], list3[:])
+        gather_split(picked_users[:, 1, :], user_planes[1], list3)
+        gather("V", picked_users[:, 2, :], user_planes[2], list3[:])
         gather_split(picked_users[:, last, :], user_planes[last], list3)
-        g1_first = held.tile([P, 1, BLK, PACK], F32, name="g1_first", tag="users1", align_bytes=64)
-        g1_rest = held.tile([P, NBLK - 2, BLK, PACK], F32, name="g1_rest", tag="users%d" % last, align_bytes=64)
-        g1 = [g1_first[:, 0]] + [g1_rest[:, n] for n in range(NBLK - 2)]
+        g1_first = held.tile([P, 2, BLK, PACK], F32, name="g1_first", tag="users1", align_bytes=64)
+        g1_rest = held.tile([P, 1, BLK, PACK], F32, name="g1_rest", tag="users%d" % last, align_bytes=64)
+        g1 = [g1_first[:, 0], g1_first[:, 1], g1_rest[:, 0]]
         for jb in range(NBLK):
             bank = table_products(notes_mx, jb)
             if jb < NBLK - 1:
@@ -167,17 +168,14 @@ def tile_attend_tab_larger_twostores_pl_kernel(
             bank = table_products(users_mx, jb)
             cols = slice((jb % 2) * BLK, (jb % 2 + 1) * BLK)
             nc.vector.tensor_tensor(g0[jb // 2][:, 0, cols], bank[:].rearrange("p r j -> p j r"), g1[jb], MAX)
-        gr = []
-        gr_mx = []
-        spread = factors[:, :, :PACK].rearrange("p k (o r) -> p k o r", o=1).to_broadcast([P, 2, HALF, PACK])
+        spread = factors[:, :, :PACK].rearrange("p k (o r) -> p k o r", o=1)
+        gr_mx = [None, None]
 
-        def weigh(h, tag):
-            gr.append(held.tile([P, 2, HALF, PACK], BF16, name="gr_%d" % h, tag=tag, align_bytes=64))
-            nc.vector.tensor_tensor(gr[h][:], g0[h][:].to_broadcast([P, 2, HALF, PACK]), spread, MULT)
-
-        def quantise_weights(h, tag):
-            gr_mx.append(mx_tiles("gr%d" % h, N, tag))
-            quantise(gr_mx[h], slice(0, N), gr[h][:].rearrange("p k c t -> p (k c t)"))
+        def weigh(name, h, cols, tag):
+            shape = [P, 2, cols.stop - cols.start, PACK]
+            gr = held.tile(shape, BF16, name=name, tag=tag, align_bytes=64)
+            nc.vector.tensor_tensor(gr[:], g0[h][:, :, cols].to_broadcast(shape), spread.to_broadcast(shape), MULT)
+            return gr
 
         def pick_values(name, plane, lst, engine, tag):
             picked = held.tile([P, N], BF16, name=name + "_picked", tag=tag, align_bytes=64)
@@ -209,65 +207,73 @@ def tile_attend_tab_larger_twostores_pl_kernel(
         out_banks = [table_psum.tile([P, 2, HALF], F32, name="table_bank") for t in range(last)]
         last_banks = [table_psum.tile([P, HALF], F32, name="table_bank"), last_psum.tile([P, HALF], F32, name="last_bank")]
 
-        def out_pass(t, h, vt, n, k):
-            cols = slice(k * HALF, (k + 1) * HALF)
+        def out_pass(t, piece, vt, n, k):
+            h, first, width = pieces[piece]
+            cols = slice(2 * first + k * width, 2 * first + (k + 1) * width)
             rows = slice(n * BLK, (n + 1) * BLK)
+            bank = last_banks[h][:] if t == last else out_banks[t][:, h]
             nc.tensor.matmul_mx(
-                out=last_banks[h][:] if t == last else out_banks[t][:, h],
+                out=bank[:, first : first + width],
                 lhsT=vt[0][:, rows].bitcast(FP8X4),
                 lhsT_scale=vt[1][:, rows],
                 rhs=gr_mx[h][0][:, cols].bitcast(FP8X4),
                 rhs_scale=gr_mx[h][1][:, cols],
-                start=k == 1 and (t == last or h == 0),
-                stop=k == 0 and (t == last or h == 1),
+                start=k == 1 and first == 0 and (t == last or h == 0),
+                stop=k == 0 and first + width == HALF and (t == last or h == 1),
             )
 
+        pieces = [(0, 0, HALF), (1, 0, BLK), (1, BLK, BLK)]
         picked2 = [
             pick_values("vt2_0", val2_planes[0], list4, "S", "vt2_0_picked"),
             pick_values("vt2_1", val2_planes[1], list4, "S", "vt2_1_picked"),
         ]
         turned = turn(picked2)
-        weigh(0, "gr_0")
-        quantise_weights(0, None)
+        gr = weigh("gr_0", 0, slice(0, HALF), "gr_0")
+        gr_mx[0] = mx_tiles("gr0", N)
+        quantise(gr_mx[0], slice(0, N), gr[:].rearrange("p k c t -> p (k c t)"))
         val2_mx = [weave_turned("S", "vt2_a", turned, 2, "vals2_2")]
         picked2 = [pick_values("vt2_%d" % t, val2_planes[t], list4, "S", "vt2_%d_picked" % t) for t in range(2, PACK)]
         turned = turn(picked2)
         picked1 = pick_values("vt1_0", val1_planes[0], list1, "S", "vt1_0_picked")
-        weigh(1, "vals2_2")
+        gr_a = weigh("gr_1a", 1, slice(0, BLK), "vals2_2")
         val2_mx.append(weave_turned("S", "vt2_b", turned, 2, "vals1_0"))
+        gr_b = weigh("gr_1b", 1, slice(BLK, HALF), "vals1_0")
         out_rows = out_0.rearrange("(p t) j -> p t j", t=PACK)
         turned0 = turn([picked1])
         picked1 = pick_values("vt1_1", val1_planes[1], list1, "S", "vt1_1_picked")
+        val1_mx = [weave_turned("S", "vt1_0", turned0, 1, "vals1_1")]
         turned1 = turn([picked1])
-        quantise_weights(1, None)
+        gr_mx[1] = mx_tiles("gr1", N, None)
+        for n, gr in enumerate((gr_a, gr_b)):
+            quantise(gr_mx[1], slice(n * HALF, (n + 1) * HALF), gr[:].rearrange("p k c t -> p (k c t)"))
         picked1 = pick_values("vt1_2", val1_planes[2], list1, "S", "vt1_2_picked")
         turned2 = turn([picked1])
         picked1 = pick_values("vt1_3", val1_planes[3], list1, "V", "vt1_3_picked")
         turned3 = turn([picked1])
-        middle_mx = mx_tiles("vt1_middle", 3 * BLK, "vals1_3")
-        val1_mx = [weave_turned("S", "vt1_0", turned0, 1, "vals1_1", middle_mx, 2)]
+        middle_mx = mx_tiles("vt1_middle", 2 * BLK, "vals1_3")
         val1_mx.append(weave_turned("S", "vt1_1", turned1, 1, "vals1_2", middle_mx, 0))
         val1_mx.append(weave_turned("S", "vt1_2", turned2, 1, "vt1_2_woven", middle_mx, 1))
         val1_mx.append(weave_turned("S", "vt1_3", turned3, 1, "vt1_3_woven"))
         result = held.tile([P, PACK, N], F32, name="result", tag="vt1_3_picked", align_bytes=64)
         for t in range(PACK):
-            for h in range(2):
+            for h in range(3):
                 out_pass(t, h, val2_mx[t // 2], t % 2, 1)
         for t in range(PACK):
-            for h in range(2):
-                out_pass(t, h, val1_mx[t], (2, 0, 1, 0)[t], 0)
+            for h in range(3):
+                out_pass(t, h, val1_mx[t], 1 if t == 2 else 0, 0)
         for t in range(last):
-            copy("VVS"[t], result[:, t, :], out_banks[t][:].rearrange("p h j -> p (h j)"))
-        nc.sync.dma_start(out_rows[:, :last, :], result[:, :last, :])
+            copy("VSS"[t], result[:, t, :], out_banks[t][:].rearrange("p h j -> p (h j)"))
+            nc.sync.dma_start(out_rows[:, t, :], result[:, t, :])
 
         woven_out = held.tile([P, N, PACK], BF16, name="woven_out", align_bytes=64)
         out_mx = mx_tiles("out", N)
         out_words = out_1[0].rearrange("p c r -> p (c r)").bitcast(I32)
         for h, cols in enumerate(halves):
             nc.scalar.copy(result[:, last, cols], last_banks[h][:])
-        nc.scalar.dma_start(out_rows[:, last, :], result[:, last, :])
-        for cols in halves:
-            weave("V", woven_out, result, cols)
+        nc.sync.dma_start(out_rows[:, last, :], result[:, last, :])
+        weave("V", woven_out, result, halves[0])
+        weave("V", woven_out, result, slice(HALF, HALF + BLK))
+        weave("S", woven_out, result, slice(HALF + BLK, N))
         for cols in halves:
             quantise(out_mx, cols, woven_out[:, cols, :].rearrange("p c t -> p (c t)"))
             nc.sync.dma_start(out_words[:, cols], out_mx[0][:, cols].bitcast(I32))

@@ -193,8 +193,9 @@ def tile_attend_tab_larger_twostores_pl_kernel(
                     nc.tensor.transpose(turned[:, n, u, :], words[:, u : HALF : 2], identity[:])
             return turned
 
-        def weave_turned(engine, name, turned, count, tag, mx=None, first=0):
-            woven = held.tile([P, count * BLK * PACK], BF16, name=name + "_woven", tag=tag, align_bytes=64)
+        def weave_turned(engine, name, turned, count, tag, mx=None, first=0, woven=None):
+            if woven is None:
+                woven = held.tile([P, count * BLK * PACK], BF16, name=name + "_woven", tag=tag, align_bytes=64)
             copy(
                 engine,
                 woven[:].bitcast(F32).rearrange("p (n e u) -> p n e u", n=count, u=2),
@@ -223,46 +224,50 @@ def tile_attend_tab_larger_twostores_pl_kernel(
             )
 
         pieces = [(0, 0, HALF), (1, 0, BLK), (1, BLK, BLK)]
-        picked2 = [
-            pick_values("vt2_0", val2_planes[0], list4, "S", "vt2_0_picked"),
-            pick_values("vt2_1", val2_planes[1], list4, "S", "vt2_1_picked"),
-        ]
-        turned = turn(picked2)
+        picked2 = [pick_values("vt2_%d" % t, val2_planes[t], list4, "S", "vt2_%d_picked" % t) for t in range(2)]
+        turned_a = turn(picked2)
         gr = weigh("gr_0", 0, slice(0, HALF), "gr_0")
         gr_mx[0] = mx_tiles("gr0", N)
         quantise(gr_mx[0], slice(0, N), gr[:].rearrange("p k c t -> p (k c t)"))
-        val2_mx = [weave_turned("S", "vt2_a", turned, 2, "vals2_2")]
         picked2 = [pick_values("vt2_%d" % t, val2_planes[t], list4, "S", "vt2_%d_picked" % t) for t in range(2, PACK)]
         turned = turn(picked2)
         picked1 = pick_values("vt1_0", val1_planes[0], list1, "S", "vt1_0_picked")
-        gr_a = weigh("gr_1a", 1, slice(0, BLK), "vals2_2")
-        val2_mx.append(weave_turned("S", "vt2_b", turned, 2, "vals1_0"))
-        gr_b = weigh("gr_1b", 1, slice(BLK, HALF), "vals1_0")
-        out_rows = out_0.rearrange("(p t) j -> p t j", t=PACK)
         turned0 = turn([picked1])
+        val2_mx = mx_tiles("vt2", N, "vt1_0_picked")
+        weave_turned("S", "vt2_a", turned_a, 2, "vals2_3", val2_mx, 0)
+        gr_a = weigh("gr_1a", 1, slice(0, BLK), "gr_1a")
+        weave_turned("S", "vt2_b", turned, 2, "vals1_0", val2_mx, 2)
+        gr_mx[1] = mx_tiles("gr1", N, None)
+        quantise(gr_mx[1], slice(0, HALF), gr_a[:].rearrange("p k c t -> p (k c t)"))
+        gr_b = weigh("gr_1b", 1, slice(BLK, HALF), "vals1_0")
+        quantise(gr_mx[1], slice(HALF, N), gr_b[:].rearrange("p k c t -> p (k c t)"))
+        out_rows = out_0.rearrange("(p t) j -> p t j", t=PACK)
         picked1 = pick_values("vt1_1", val1_planes[1], list1, "S", "vt1_1_picked")
         val1_mx = [weave_turned("S", "vt1_0", turned0, 1, "vals1_1")]
         turned1 = turn([picked1])
-        gr_mx[1] = mx_tiles("gr1", N, None)
-        for n, gr in enumerate((gr_a, gr_b)):
-            quantise(gr_mx[1], slice(n * HALF, (n + 1) * HALF), gr[:].rearrange("p k c t -> p (k c t)"))
         picked1 = pick_values("vt1_2", val1_planes[2], list1, "S", "vt1_2_picked")
         turned2 = turn([picked1])
-        picked1 = pick_values("vt1_3", val1_planes[3], list1, "V", "vt1_3_picked")
+        picked1 = pick_values("vt1_3", val1_planes[3], list1, "B", "vt1_3_picked")
         turned3 = turn([picked1])
-        middle_mx = mx_tiles("vt1_middle", 2 * BLK, "vals1_3")
-        val1_mx.append(weave_turned("S", "vt1_1", turned1, 1, "vals1_2", middle_mx, 0))
-        val1_mx.append(weave_turned("S", "vt1_2", turned2, 1, "vt1_2_woven", middle_mx, 1))
+        middle = held.tile([P, 2, N], BF16, name="middle_woven", tag="vals1_3", align_bytes=64)
+        middle_mx = mx_tiles("vt1_middle", 2 * BLK)
+        val1_mx.append(weave_turned("V", "vt1_1", turned1, 1, None, middle_mx, 0, middle[:, 0]))
+        val1_mx.append(weave_turned("S", "vt1_2", turned2, 1, None, middle_mx, 1, middle[:, 1]))
         val1_mx.append(weave_turned("S", "vt1_3", turned3, 1, "vt1_3_woven"))
         result = held.tile([P, PACK, N], F32, name="result", tag="vt1_3_picked", align_bytes=64)
+        for h in range(2):
+            for t in range(PACK):
+                out_pass(t, h, val2_mx, t, 1)
+        for t in range(1):
+            for h in range(2):
+                out_pass(t, h, val1_mx[t], 1 if t == 2 else 0, 0)
         for t in range(PACK):
-            for h in range(3):
-                out_pass(t, h, val2_mx[t // 2], t % 2, 1)
+            out_pass(t, 2, val2_mx, t, 1)
         for t in range(PACK):
-            for h in range(3):
+            for h in range(2 if t < 1 else 0, 3):
                 out_pass(t, h, val1_mx[t], 1 if t == 2 else 0, 0)
         for t in range(last):
-            copy("VSS"[t], result[:, t, :], out_banks[t][:].rearrange("p h j -> p (h j)"))
+            copy("SVV"[t], result[:, t, :], out_banks[t][:].rearrange("p h j -> p (h j)"))
             nc.sync.dma_start(out_rows[:, t, :], result[:, t, :])
 
         woven_out = held.tile([P, N, PACK], BF16, name="woven_out", align_bytes=64)

@@ -14,14 +14,19 @@ FP4X4 = mybir.dt.float4_e2m1fn_x4
 COPY = mybir.ActivationFunctionType.Copy
 MAX = mybir.AluOpType.max
 MULT = mybir.AluOpType.mult
+VECTOR, SCALAR = "vector", "scalar"
 
 P = 128
 PACK = 4
+LAST = PACK - 1
 N = 512
 BLK = 128
 NBLK = N // BLK
 HALF = N // 2
 LIST_COLS = N // 16
+QUADRANTS = 4
+RUN = 4
+TURN_BANKS = 3
 
 FLOPS = 4 * 2 * 512 * 512 * 512
 
@@ -31,11 +36,12 @@ def tile_attend_tab_larger_twostores_pl_kernel(
 ):
     nc = tc.nc
     tokens = keys_scales.shape[2]
+    halves = [slice(0, HALF), slice(HALF, N)]
 
     with ExitStack() as ctx:
         held = ctx.enter_context(tc.tile_pool(name="held", bufs=1))
         table_psum = ctx.enter_context(tc.psum_pool(name="table_psum", bufs=NBLK))
-        turn_psum = ctx.enter_context(tc.psum_pool(name="turn_psum", bufs=3))
+        turn_psum = ctx.enter_context(tc.psum_pool(name="turn_psum", bufs=TURN_BANKS))
         last_psum = ctx.enter_context(tc.psum_pool(name="last_psum", bufs=1))
 
         def load_list(name, src):
@@ -43,23 +49,23 @@ def tile_attend_tab_larger_twostores_pl_kernel(
             nc.sync.dma_start(lst[:], src)
             return lst
 
-        def load_plane(name, pool, t):
-            plane = held.tile([P, pool.shape[1]], F32, name="%s%d" % (name, t), tag="%s%d" % (name, t), align_bytes=64)
-            nc.sync.dma_start(plane[:], pool.rearrange("(p t) c -> t p c", t=PACK)[t])
+        def load_plane(name, src, t):
+            plane = held.tile([P, src.shape[1]], F32, name="%s%d" % (name, t), tag="%s%d" % (name, t), align_bytes=64)
+            nc.sync.dma_start(plane[:], src.rearrange("(p t) c -> t p c", t=PACK)[t])
             return plane
 
         def gather(engine, dst, plane, lst):
-            if engine == "V":
+            if engine == VECTOR:
                 nc.vector.tensor_copy(dst, plane[:].indirect(lst))
             else:
                 nc.scalar.activation(dst, plane[:].indirect(lst), COPY)
 
         def gather_split(dst, plane, lst):
-            gather("V", dst[:, :HALF], plane, lst[:, : LIST_COLS // 2])
-            gather("S", dst[:, HALF:], plane, lst[:, LIST_COLS // 2 :])
+            gather(VECTOR, dst[:, :HALF], plane, lst[:, : LIST_COLS // 2])
+            gather(SCALAR, dst[:, HALF:], plane, lst[:, LIST_COLS // 2 :])
 
         def copy(engine, dst, src):
-            if engine == "V":
+            if engine == VECTOR:
                 nc.vector.tensor_copy(dst, src)
             else:
                 nc.scalar.copy(dst, src)
@@ -72,13 +78,20 @@ def tile_attend_tab_larger_twostores_pl_kernel(
         def quantise(mx, cols, woven):
             nc.vector.quantize_mx(out=mx[0][:, cols].bitcast(FP8X4), scales=mx[1][:, cols], in_=woven)
 
+        def weave(engine, woven, planes, cols):
+            copy(
+                engine,
+                woven[:, cols, :].rearrange("p (c i) t -> p c t i", i=RUN),
+                planes[:, :, cols].rearrange("p t (c i) -> p c t i", i=RUN),
+            )
+
         list2 = load_list("list2", offs2)
         note_planes = [load_plane("notes", notes, 0)]
         key_words = held.tile([P, tokens], U16, name="key_words")
         nc.sync.dma_start(key_words[:].bitcast(I32), keys_words[0].bitcast(I32))
         key_bytes = held.tile([P, tokens], U8, name="key_bytes")
         nc.gpsimd.memset(key_bytes[:].bitcast(I32), 0)
-        for q in range(4):
+        for q in range(QUADRANTS):
             nc.scalar.dma_start(
                 key_bytes[32 * q : 32 * q + 4, :].bitcast(I32), keys_scales[0, 4 * q : 4 * q + 4, :].bitcast(I32)
             )
@@ -88,13 +101,13 @@ def tile_attend_tab_larger_twostores_pl_kernel(
         list3 = load_list("list3", offs3)
         user_planes.extend(load_plane("users", users2, t) for t in range(1, PACK))
         list4 = load_list("list4", offs4)
-        factors = held.tile([P, 2, 2 * PACK], F32, name="factors")
-        for k, src in enumerate((rowf, rowf2)):
-            nc.sync.dma_start(factors[:, k, :PACK], src.rearrange("(p r) o -> p (r o)", r=PACK))
         val2_planes = [load_plane("vals2_", vals2, t) for t in range(PACK)]
         val1_planes = [load_plane("vals1_", vals, t) for t in range(PACK)]
         identity = held.tile([P, P], F32, name="identity")
         make_identity(nc, identity[:])
+        factors = held.tile([P, 2, 2 * PACK], F32, name="factors")
+        for k, src in enumerate((rowf, rowf2)):
+            nc.gpsimd.dma_start(factors[:, k, :PACK], src.rearrange("(p r) o -> p (r o)", r=PACK))
 
         picked_words = held.tile([P, N], U16, name="picked_words")
         nc.vector.tensor_copy(picked_words[:], key_words[:].indirect(list1[:]))
@@ -102,13 +115,6 @@ def tile_attend_tab_larger_twostores_pl_kernel(
         nc.vector.tensor_copy(dealt_words[:], picked_words[:].rearrange("p (s r) -> p r s", r=PACK))
         dealt_bytes = held.tile([P, PACK, BLK], U8, name="dealt_bytes", align_bytes=64)
         nc.vector.tensor_copy(dealt_bytes[:].rearrange("p r s -> p s r"), key_bytes[:].indirect(list1[:]))
-
-        def weave(engine, woven, picked, cols):
-            copy(
-                engine,
-                woven[:, cols, :].rearrange("p (c i) t -> p c t i", i=4),
-                picked[:, :, cols].rearrange("p t (c i) -> p c t i", i=4),
-            )
 
         def table_products(mx, jb):
             bank = table_psum.tile([P, PACK, BLK], F32, name="table_bank")
@@ -125,64 +131,68 @@ def tile_attend_tab_larger_twostores_pl_kernel(
                 )
             return bank
 
-        halves = [slice(0, HALF), slice(HALF, N)]
-
-        last = PACK - 1
-
         picked_notes = held.tile([P, PACK, N], BF16, name="picked_notes")
-        for t in range(last):
-            gather("S", picked_notes[:, t, :], note_planes[t], list2[:])
-        gather_split(picked_notes[:, last, :], note_planes[last], list2)
+        for t in range(LAST):
+            gather(SCALAR, picked_notes[:, t, :], note_planes[t], list2[:])
+        gather_split(picked_notes[:, LAST, :], note_planes[LAST], list2)
         woven_notes = held.tile([P, N, PACK], BF16, name="woven_notes", align_bytes=64)
         notes_mx = mx_tiles("notes", N)
         for cols in halves:
-            weave("V", woven_notes, picked_notes, cols)
+            weave(VECTOR, woven_notes, picked_notes, cols)
         for cols in halves:
             quantise(notes_mx, cols, woven_notes[:, cols, :].rearrange("p c t -> p (c t)"))
-        picked_users = held.tile([P, PACK, N], BF16, name="picked_users", tag="picked_users", align_bytes=64)
-        gather("S", picked_users[:, 0, :], user_planes[0], list3[:])
+
+        picked_users = held.tile([P, PACK, N], BF16, name="picked_users", align_bytes=64)
+        gather(SCALAR, picked_users[:, 0, :], user_planes[0], list3[:])
         gather_split(picked_users[:, 1, :], user_planes[1], list3)
-        gather("V", picked_users[:, 2, :], user_planes[2], list3[:])
-        gather_split(picked_users[:, last, :], user_planes[last], list3)
+        gather(VECTOR, picked_users[:, 2, :], user_planes[2], list3[:])
+        gather_split(picked_users[:, LAST, :], user_planes[LAST], list3)
+
         g1_first = held.tile([P, 2, BLK, PACK], F32, name="g1_first", tag="users1", align_bytes=64)
-        g1_rest = held.tile([P, 1, BLK, PACK], F32, name="g1_rest", tag="users%d" % last, align_bytes=64)
+        g1_rest = held.tile([P, 1, BLK, PACK], F32, name="g1_rest", tag="users%d" % LAST, align_bytes=64)
         g1 = [g1_first[:, 0], g1_first[:, 1], g1_rest[:, 0]]
-        for jb in range(NBLK):
-            bank = table_products(notes_mx, jb)
-            if jb < NBLK - 1:
-                nc.scalar.copy(g1[jb], bank[:].rearrange("p r j -> p j r"))
+        for jb in range(NBLK - 1):
+            nc.scalar.copy(g1[jb], table_products(notes_mx, jb)[:].rearrange("p r j -> p j r"))
+        g1_last_bank = table_products(notes_mx, NBLK - 1)
 
         woven_users = held.tile([P, N, PACK], BF16, name="woven_users", tag="woven_users", align_bytes=64)
         users_mx = mx_tiles("users", N)
         for cols in halves:
-            weave("V", woven_users, picked_users, cols)
+            weave(VECTOR, woven_users, picked_users, cols)
         for cols in halves:
             quantise(users_mx, cols, woven_users[:, cols, :].rearrange("p c t -> p (c t)"))
 
         g1_last = held.tile([P, BLK, PACK], F32, name="g1_last", tag="woven_users", align_bytes=64)
-        nc.vector.tensor_copy(g1_last[:], bank[:].rearrange("p r j -> p j r"))
+        nc.vector.tensor_copy(g1_last[:], g1_last_bank[:].rearrange("p r j -> p j r"))
         g1.append(g1_last[:])
 
-        g0 = [held.tile([P, 1, HALF, PACK], F32, name="g0_%d" % h, tag="g0_%d" % h, align_bytes=64) for h in range(2)]
+        g0 = [held.tile([P, 1, HALF, PACK], F32, name="g0_%d" % h, align_bytes=64) for h in range(2)]
         for jb in range(NBLK):
             bank = table_products(users_mx, jb)
             cols = slice((jb % 2) * BLK, (jb % 2 + 1) * BLK)
             nc.vector.tensor_tensor(g0[jb // 2][:, 0, cols], bank[:].rearrange("p r j -> p j r"), g1[jb], MAX)
         spread = factors[:, :, :PACK].rearrange("p k (o r) -> p k o r", o=1)
-        gr_mx = [None, None]
 
-        def weigh(name, h, cols, tag):
-            shape = [P, 2, cols.stop - cols.start, PACK]
+        pieces = [(0, 0, HALF), (1, 0, BLK), (1, BLK, BLK)]
+
+        def weigh(name, piece, tag):
+            h, first, width = pieces[piece]
+            shape = [P, 2, width, PACK]
             gr = held.tile(shape, BF16, name=name, tag=tag, align_bytes=64)
-            nc.vector.tensor_tensor(gr[:], g0[h][:, :, cols].to_broadcast(shape), spread.to_broadcast(shape), MULT)
+            table = g0[h][:, :, first : first + width].to_broadcast(shape)
+            nc.vector.tensor_tensor(gr[:], table, spread.to_broadcast(shape), MULT)
             return gr
 
-        def pick_values(name, plane, lst, engine, tag):
-            picked = held.tile([P, N], BF16, name=name + "_picked", tag=tag, align_bytes=64)
-            if engine == "B":
-                gather_split(picked[:], plane, lst)
-            else:
-                gather(engine, picked[:], plane, lst[:])
+        def quantise_weights(piece, gr):
+            h, first, width = pieces[piece]
+            quantise(gr_mx[h], slice(2 * first, 2 * (first + width)), gr[:].rearrange("p k c t -> p (k c t)"))
+
+        def picked_tile(name):
+            return held.tile([P, N], BF16, name=name + "_picked", tag=name + "_picked", align_bytes=64)
+
+        def pick_values(name, plane, lst):
+            picked = picked_tile(name)
+            gather(SCALAR, picked[:], plane, lst[:])
             return picked
 
         def turn(group):
@@ -193,96 +203,100 @@ def tile_attend_tab_larger_twostores_pl_kernel(
                     nc.tensor.transpose(turned[:, n, u, :], words[:, u : HALF : 2], identity[:])
             return turned
 
-        def weave_turned(engine, name, turned, count, tag, mx=None, first=0, woven=None):
-            if woven is None:
-                woven = held.tile([P, count * BLK * PACK], BF16, name=name + "_woven", tag=tag, align_bytes=64)
+        def woven_tile(name, count, tag):
+            return held.tile([P, count * BLK * PACK], BF16, name=name + "_woven", tag=tag, align_bytes=64)[:]
+
+        def weave_turned(engine, woven, turned, mx, first):
+            count = turned.shape[1]
             copy(
                 engine,
-                woven[:].bitcast(F32).rearrange("p (n e u) -> p n e u", n=count, u=2),
+                woven.bitcast(F32).rearrange("p (n e u) -> p n e u", n=count, u=2),
                 turned[:].rearrange("p n u e -> p n e u"),
             )
-            mx = mx or mx_tiles(name, count * BLK)
-            quantise(mx, slice(first * BLK, (first + count) * BLK), woven[:])
-            return mx
+            quantise(mx, slice(first * BLK, (first + count) * BLK), woven)
 
-        out_banks = [table_psum.tile([P, 2, HALF], F32, name="table_bank") for t in range(last)]
+        out_banks = [table_psum.tile([P, 2, HALF], F32, name="table_bank") for t in range(LAST)]
         last_banks = [table_psum.tile([P, HALF], F32, name="table_bank"), last_psum.tile([P, HALF], F32, name="last_bank")]
 
         def out_pass(t, piece, vt, n, k):
             h, first, width = pieces[piece]
             cols = slice(2 * first + k * width, 2 * first + (k + 1) * width)
             rows = slice(n * BLK, (n + 1) * BLK)
-            bank = last_banks[h][:] if t == last else out_banks[t][:, h]
+            bank = last_banks[h][:] if t == LAST else out_banks[t][:, h]
             nc.tensor.matmul_mx(
                 out=bank[:, first : first + width],
                 lhsT=vt[0][:, rows].bitcast(FP8X4),
                 lhsT_scale=vt[1][:, rows],
                 rhs=gr_mx[h][0][:, cols].bitcast(FP8X4),
                 rhs_scale=gr_mx[h][1][:, cols],
-                start=k == 1 and first == 0 and (t == last or h == 0),
-                stop=k == 0 and first + width == HALF and (t == last or h == 1),
+                start=k == 1 and first == 0 and (t == LAST or h == 0),
+                stop=k == 0 and first + width == HALF and (t == LAST or h == 1),
             )
 
-        pieces = [(0, 0, HALF), (1, 0, BLK), (1, BLK, BLK)]
-        picked2 = [pick_values("vt2_%d" % t, val2_planes[t], list4, "S", "vt2_%d_picked" % t) for t in range(2)]
-        turned_a = turn(picked2)
-        gr = weigh("gr_0", 0, slice(0, HALF), "gr_0")
-        gr_mx[0] = mx_tiles("gr0", N)
-        quantise(gr_mx[0], slice(0, N), gr[:].rearrange("p k c t -> p (k c t)"))
-        picked2 = [pick_values("vt2_%d" % t, val2_planes[t], list4, "S", "vt2_%d_picked" % t) for t in range(2, PACK)]
-        turned = turn(picked2)
-        picked1 = pick_values("vt1_0", val1_planes[0], list1, "S", "vt1_0_picked")
-        turned0 = turn([picked1])
+        turned2_low = turn([pick_values("vt2_%d" % t, val2_planes[t], list4) for t in range(2)])
+        gr = weigh("gr_0", 0, "gr_0")
+        gr_mx = [mx_tiles("gr0", N)]
+        quantise_weights(0, gr)
+        turned2_high = turn([pick_values("vt2_%d" % t, val2_planes[t], list4) for t in range(2, PACK)])
+        turned1 = [turn([pick_values("vt1_0", val1_planes[0], list1)])]
         val2_mx = mx_tiles("vt2", N, "vt1_0_picked")
-        weave_turned("S", "vt2_a", turned_a, 2, "vals2_3", val2_mx, 0)
-        gr_a = weigh("gr_1a", 1, slice(0, BLK), "gr_1a")
-        weave_turned("S", "vt2_b", turned, 2, "vals1_0", val2_mx, 2)
-        gr_mx[1] = mx_tiles("gr1", N, None)
-        quantise(gr_mx[1], slice(0, HALF), gr_a[:].rearrange("p k c t -> p (k c t)"))
-        gr_b = weigh("gr_1b", 1, slice(BLK, HALF), "vals1_0")
-        quantise(gr_mx[1], slice(HALF, N), gr_b[:].rearrange("p k c t -> p (k c t)"))
-        out_rows = out_0.rearrange("(p t) j -> p t j", t=PACK)
-        picked1 = pick_values("vt1_1", val1_planes[1], list1, "S", "vt1_1_picked")
-        val1_mx = [weave_turned("S", "vt1_0", turned0, 1, "vals1_1")]
-        turned1 = turn([picked1])
-        picked1 = pick_values("vt1_2", val1_planes[2], list1, "S", "vt1_2_picked")
-        turned2 = turn([picked1])
-        picked1 = pick_values("vt1_3", val1_planes[3], list1, "B", "vt1_3_picked")
-        turned3 = turn([picked1])
-        middle = held.tile([P, 2, N], BF16, name="middle_woven", tag="vals1_3", align_bytes=64)
+        weave_turned(SCALAR, woven_tile("vt2_a", 2, "vals2_%d" % LAST), turned2_low, val2_mx, 0)
+        gr = weigh("gr_1a", 1, "gr_1a")
+        weave_turned(SCALAR, woven_tile("vt2_b", 2, "vals1_0"), turned2_high, val2_mx, 2)
+        gr_mx.append(mx_tiles("gr1", N))
+        quantise_weights(1, gr)
+        quantise_weights(2, weigh("gr_1b", 2, "vals1_0"))
+
+        picked = pick_values("vt1_1", val1_planes[1], list1)
+        woven = woven_tile("vt1_0", 1, "vals1_1")
+        first_mx = mx_tiles("vt1_0", BLK)
+        weave_turned(SCALAR, woven, turned1[0], first_mx, 0)
+        turned1.append(turn([picked]))
+        turned1.append(turn([pick_values("vt1_2", val1_planes[2], list1)]))
+        picked = picked_tile("vt1_%d" % LAST)
+        gather_split(picked[:], val1_planes[LAST], list1)
+        turned1.append(turn([picked]))
+        middle = held.tile([P, 2, N], BF16, name="middle_woven", tag="vals1_%d" % LAST, align_bytes=64)
         middle_mx = mx_tiles("vt1_middle", 2 * BLK)
-        val1_mx.append(weave_turned("V", "vt1_1", turned1, 1, None, middle_mx, 0, middle[:, 0]))
-        val1_mx.append(weave_turned("S", "vt1_2", turned2, 1, None, middle_mx, 1, middle[:, 1]))
-        val1_mx.append(weave_turned("S", "vt1_3", turned3, 1, "vt1_3_woven"))
-        result = held.tile([P, PACK, N], F32, name="result", tag="vt1_3_picked", align_bytes=64)
-        for h in range(2):
+        weave_turned(VECTOR, middle[:, 0], turned1[1], middle_mx, 0)
+        weave_turned(SCALAR, middle[:, 1], turned1[2], middle_mx, 1)
+        woven = woven_tile("vt1_3", 1, "vt1_3_woven")
+        last_mx = mx_tiles("vt1_3", BLK)
+        weave_turned(SCALAR, woven, turned1[LAST], last_mx, 0)
+        val1 = [(first_mx, 0), (middle_mx, 0), (middle_mx, 1), (last_mx, 0)]
+
+        result = held.tile([P, PACK, N], F32, name="result", tag="vt1_%d_picked" % LAST, align_bytes=64)
+        for piece in range(2):
             for t in range(PACK):
-                out_pass(t, h, val2_mx, t, 1)
-        for t in range(1):
-            for h in range(2):
-                out_pass(t, h, val1_mx[t], 1 if t == 2 else 0, 0)
+                out_pass(t, piece, val2_mx, t, 1)
+        for piece in range(2):
+            out_pass(0, piece, *val1[0], 0)
         for t in range(PACK):
             out_pass(t, 2, val2_mx, t, 1)
-        for t in range(PACK):
-            for h in range(2 if t < 1 else 0, 3):
-                out_pass(t, h, val1_mx[t], 1 if t == 2 else 0, 0)
-        for t in range(last):
-            copy("SVV"[t], result[:, t, :], out_banks[t][:].rearrange("p h j -> p (h j)"))
+        out_pass(0, 2, *val1[0], 0)
+        for t in range(1, PACK):
+            for piece in range(len(pieces)):
+                out_pass(t, piece, *val1[t], 0)
+
+        out_rows = out_0.rearrange("(p t) j -> p t j", t=PACK)
+        for t, engine in enumerate((SCALAR, SCALAR, VECTOR)):
+            copy(engine, result[:, t, :], out_banks[t][:].rearrange("p h j -> p (h j)"))
             nc.sync.dma_start(out_rows[:, t, :], result[:, t, :])
 
         woven_out = held.tile([P, N, PACK], BF16, name="woven_out", align_bytes=64)
         out_mx = mx_tiles("out", N)
         out_words = out_1[0].rearrange("p c r -> p (c r)").bitcast(I32)
         for h, cols in enumerate(halves):
-            nc.scalar.copy(result[:, last, cols], last_banks[h][:])
-        nc.sync.dma_start(out_rows[:, last, :], result[:, last, :])
-        weave("V", woven_out, result, halves[0])
-        weave("V", woven_out, result, slice(HALF, HALF + BLK))
-        weave("S", woven_out, result, slice(HALF + BLK, N))
+            nc.scalar.copy(result[:, LAST, cols], last_banks[h][:])
+        nc.sync.dma_start(out_rows[:, LAST, :], result[:, LAST, :])
+        weave(VECTOR, woven_out, result, halves[0])
+        weave(VECTOR, woven_out, result, slice(HALF, HALF + BLK))
+        weave(SCALAR, woven_out, result, slice(HALF + BLK, N))
         for cols in halves:
             quantise(out_mx, cols, woven_out[:, cols, :].rearrange("p c t -> p (c t)"))
             nc.sync.dma_start(out_words[:, cols], out_mx[0][:, cols].bitcast(I32))
-        for q in range(4):
-            nc.scalar.dma_start(
+        for q in range(QUADRANTS):
+            queue = nc.sync if q == QUADRANTS - 1 else nc.scalar
+            queue.dma_start(
                 out_2[0, 4 * q : 4 * q + 4, :].bitcast(I32), out_mx[1][32 * q : 32 * q + 4, :].bitcast(I32)
             )

from contextlib import ExitStack

import concourse.mybir as mybir
from concourse.masks import make_identity

F32 = mybir.dt.float32
BF16 = mybir.dt.bfloat16
I32 = mybir.dt.int32
U32 = mybir.dt.uint32
U16 = mybir.dt.uint16
U8 = mybir.dt.uint8
FP8X4 = mybir.dt.float8_e4m3fn_x4
FP4X4 = mybir.dt.float4_e2m1fn_x4
COPY = mybir.ActivationFunctionType.Copy
MAX = mybir.AluOpType.max
MULT = mybir.AluOpType.mult
VECTOR, SCALAR = "vector", "scalar"

P = 128
PACK = 4
LAST = PACK - 1
N = 512
BLK = 128
NBLK = N // BLK
HALF = N // 2
LIST_COLS = N // 16
QUADRANTS = 4
RUN = 4
TURN_BANKS = 3

FLOPS = 4 * 2 * 512 * 512 * 512


def tile_attend_tab_larger_twostores_pl_kernel(
    tc, keys_words, keys_scales, notes, users2, rowf, rowf2, vals, vals2, offs, offs2, offs3, offs4, out_0, out_1, out_2
):
    nc = tc.nc
    tokens = keys_scales.shape[2]
    halves = [slice(0, HALF), slice(HALF, N)]

    with ExitStack() as ctx:
        held = ctx.enter_context(tc.tile_pool(name="held", bufs=1))
        table_psum = ctx.enter_context(tc.psum_pool(name="table_psum", bufs=NBLK))
        turn_psum = ctx.enter_context(tc.psum_pool(name="turn_psum", bufs=TURN_BANKS))
        last_psum = ctx.enter_context(tc.psum_pool(name="last_psum", bufs=1))

        def load_list(name, src):
            lst = held.tile([P, LIST_COLS], U16, name=name)
            nc.sync.dma_start(lst[:], src)
            return lst

        def load_plane(name, src, t):
            plane = held.tile([P, src.shape[1]], F32, name="%s%d" % (name, t), tag="%s%d" % (name, t), align_bytes=64)
            nc.sync.dma_start(plane[:], src.rearrange("(p t) c -> t p c", t=PACK)[t])
            return plane

        def gather(engine, dst, plane, lst):
            if engine == VECTOR:
                nc.vector.tensor_copy(dst, plane[:].indirect(lst))
            else:
                nc.scalar.activation(dst, plane[:].indirect(lst), COPY)

        def gather_split(dst, plane, lst):
            gather(VECTOR, dst[:, :HALF], plane, lst[:, : LIST_COLS // 2])
            gather(SCALAR, dst[:, HALF:], plane, lst[:, LIST_COLS // 2 :])

        def copy(engine, dst, src):
            if engine == VECTOR:
                nc.vector.tensor_copy(dst, src)
            else:
                nc.scalar.copy(dst, src)

        def mx_tiles(name, width, tag=None):
            codes = held.tile([P, width], U32, name=name + "_codes", tag=tag or name + "_codes", align_bytes=64)
            scales = held.tile([P, width], U8, name=name + "_scales", align_bytes=64)
            return codes, scales

        def quantise(mx, cols, woven):
            nc.vector.quantize_mx(out=mx[0][:, cols].bitcast(FP8X4), scales=mx[1][:, cols], in_=woven)

        def weave(engine, woven, planes, cols):
            copy(
                engine,
                woven[:, cols, :].rearrange("p (c i) t -> p c t i", i=RUN),
                planes[:, :, cols].rearrange("p t (c i) -> p c t i", i=RUN),
            )

        list2 = load_list("list2", offs2)
        note_planes = [load_plane("notes", notes, 0)]
        key_words = held.tile([P, tokens], U16, name="key_words")
        nc.sync.dma_start(key_words[:].bitcast(I32), keys_words[0].bitcast(I32))
        key_bytes = held.tile([P, tokens], U8, name="key_bytes")
        nc.gpsimd.memset(key_bytes[:].bitcast(I32), 0)
        for q in range(QUADRANTS):
            nc.scalar.dma_start(
                key_bytes[32 * q : 32 * q + 4, :].bitcast(I32), keys_scales[0, 4 * q : 4 * q + 4, :].bitcast(I32)
            )
        list1 = load_list("list1", offs)
        note_planes.extend(load_plane("notes", notes, t) for t in range(1, PACK))
        user_planes = [load_plane("users", users2, 0)]
        list3 = load_list("list3", offs3)
        user_planes.extend(load_plane("users", users2, t) for t in range(1, PACK))
        list4 = load_list("list4", offs4)
        val2_planes = [load_plane("vals2_", vals2, t) for t in range(PACK)]
        val1_planes = [load_plane("vals1_", vals, t) for t in range(PACK)]
        identity = held.tile([P, P], F32, name="identity")
        make_identity(nc, identity[:])
        factors = held.tile([P, 2, 2 * PACK], F32, name="factors")
        for k, src in enumerate((rowf, rowf2)):
            nc.gpsimd.dma_start(factors[:, k, :PACK], src.rearrange("(p r) o -> p (r o)", r=PACK))

        picked_words = held.tile([P, N], U16, name="picked_words")
        nc.vector.tensor_copy(picked_words[:], key_words[:].indirect(list1[:]))
        dealt_words = held.tile([P, PACK, BLK], U16, name="dealt_words", align_bytes=64)
        nc.vector.tensor_copy(dealt_words[:], picked_words[:].rearrange("p (s r) -> p r s", r=PACK))
        dealt_bytes = held.tile([P, PACK, BLK], U8, name="dealt_bytes", align_bytes=64)
        nc.vector.tensor_copy(dealt_bytes[:].rearrange("p r s -> p s r"), key_bytes[:].indirect(list1[:]))

        def table_products(mx, jb):
            bank = table_psum.tile([P, PACK, BLK], F32, name="table_bank")
            cols = slice(jb * BLK, (jb + 1) * BLK)
            for r in range(PACK):
                nc.tensor.matmul_mx(
                    out=bank[:, r, :],
                    lhsT=dealt_words[:, r, :].bitcast(FP4X4),
                    lhsT_scale=dealt_bytes[:, r, :],
                    rhs=mx[0][:, cols].bitcast(FP8X4),
                    rhs_scale=mx[1][:, cols],
                    start=True,
                    stop=True,
                )
            return bank

        picked_notes = held.tile([P, PACK, N], BF16, name="picked_notes")
        for t in range(LAST):
            gather(SCALAR, picked_notes[:, t, :], note_planes[t], list2[:])
        gather_split(picked_notes[:, LAST, :], note_planes[LAST], list2)
        woven_notes = held.tile([P, N, PACK], BF16, name="woven_notes", align_bytes=64)
        notes_mx = mx_tiles("notes", N)
        for cols in halves:
            weave(VECTOR, woven_notes, picked_notes, cols)
        for cols in halves:
            quantise(notes_mx, cols, woven_notes[:, cols, :].rearrange("p c t -> p (c t)"))

        picked_users = held.tile([P, PACK, N], BF16, name="picked_users", align_bytes=64)
        gather(SCALAR, picked_users[:, 0, :], user_planes[0], list3[:])
        gather_split(picked_users[:, 1, :], user_planes[1], list3)
        gather(VECTOR, picked_users[:, 2, :], user_planes[2], list3[:])
        gather_split(picked_users[:, LAST, :], user_planes[LAST], list3)

        g1_first = held.tile([P, 2, BLK, PACK], F32, name="g1_first", tag="users1", align_bytes=64)
        g1_rest = held.tile([P, 1, BLK, PACK], F32, name="g1_rest", tag="users%d" % LAST, align_bytes=64)
        g1 = [g1_first[:, 0], g1_first[:, 1], g1_rest[:, 0]]
        for jb in range(NBLK - 1):
            nc.scalar.copy(g1[jb], table_products(notes_mx, jb)[:].rearrange("p r j -> p j r"))
        g1_last_bank = table_products(notes_mx, NBLK - 1)

        woven_users = held.tile([P, N, PACK], BF16, name="woven_users", tag="woven_users", align_bytes=64)
        users_mx = mx_tiles("users", N)
        for cols in halves:
            weave(VECTOR, woven_users, picked_users, cols)
        for cols in halves:
            quantise(users_mx, cols, woven_users[:, cols, :].rearrange("p c t -> p (c t)"))

        g1_last = held.tile([P, BLK, PACK], F32, name="g1_last", tag="woven_users", align_bytes=64)
        nc.vector.tensor_copy(g1_last[:], g1_last_bank[:].rearrange("p r j -> p j r"))
        g1.append(g1_last[:])

        g0 = [held.tile([P, 1, HALF, PACK], F32, name="g0_%d" % h, align_bytes=64) for h in range(2)]
        for jb in range(NBLK):
            bank = table_products(users_mx, jb)
            cols = slice((jb % 2) * BLK, (jb % 2 + 1) * BLK)
            nc.vector.tensor_tensor(g0[jb // 2][:, 0, cols], bank[:].rearrange("p r j -> p j r"), g1[jb], MAX)
        spread = factors[:, :, :PACK].rearrange("p k (o r) -> p k o r", o=1)

        pieces = [(0, 0, HALF), (1, 0, BLK), (1, BLK, BLK)]

        def weigh(name, piece, tag):
            h, first, width = pieces[piece]
            shape = [P, 2, width, PACK]
            gr = held.tile(shape, BF16, name=name, tag=tag, align_bytes=64)
            table = g0[h][:, :, first : first + width].to_broadcast(shape)
            nc.vector.tensor_tensor(gr[:], table, spread.to_broadcast(shape), MULT)
            return gr

        def quantise_weights(piece, gr):
            h, first, width = pieces[piece]
            quantise(gr_mx[h], slice(2 * first, 2 * (first + width)), gr[:].rearrange("p k c t -> p (k c t)"))

        def picked_tile(name):
            return held.tile([P, N], BF16, name=name + "_picked", tag=name + "_picked", align_bytes=64)

        def pick_values(name, plane, lst):
            picked = picked_tile(name)
            gather(SCALAR, picked[:], plane, lst[:])
            return picked

        def turn(group):
            turned = turn_psum.tile([P, len(group), 2, BLK], F32, name="turned")
            for n, picked in enumerate(group):
                words = picked[:].bitcast(F32)
                for u in range(2):
                    nc.tensor.transpose(turned[:, n, u, :], words[:, u : HALF : 2], identity[:])
            return turned

        def woven_tile(name, count, tag):
            return held.tile([P, count * BLK * PACK], BF16, name=name + "_woven", tag=tag, align_bytes=64)[:]

        def weave_turned(engine, woven, turned, mx, first):
            count = turned.shape[1]
            copy(
                engine,
                woven.bitcast(F32).rearrange("p (n e u) -> p n e u", n=count, u=2),
                turned[:].rearrange("p n u e -> p n e u"),
            )
            quantise(mx, slice(first * BLK, (first + count) * BLK), woven)

        out_banks = [table_psum.tile([P, 2, HALF], F32, name="table_bank") for t in range(LAST)]
        last_banks = [table_psum.tile([P, HALF], F32, name="table_bank"), last_psum.tile([P, HALF], F32, name="last_bank")]

        def out_pass(t, piece, vt, n, k):
            h, first, width = pieces[piece]
            cols = slice(2 * first + k * width, 2 * first + (k + 1) * width)
            rows = slice(n * BLK, (n + 1) * BLK)
            bank = last_banks[h][:] if t == LAST else out_banks[t][:, h]
            nc.tensor.matmul_mx(
                out=bank[:, first : first + width],
                lhsT=vt[0][:, rows].bitcast(FP8X4),
                lhsT_scale=vt[1][:, rows],
                rhs=gr_mx[h][0][:, cols].bitcast(FP8X4),
                rhs_scale=gr_mx[h][1][:, cols],
                start=k == 1 and first == 0 and (t == LAST or h == 0),
                stop=k == 0 and first + width == HALF and (t == LAST or h == 1),
            )

        turned2_low = turn([pick_values("vt2_%d" % t, val2_planes[t], list4) for t in range(2)])
        gr = weigh("gr_0", 0, "gr_0")
        gr_mx = [mx_tiles("gr0", N)]
        quantise_weights(0, gr)
        turned2_high = turn([pick_values("vt2_%d" % t, val2_planes[t], list4) for t in range(2, PACK)])
        turned1 = [turn([pick_values("vt1_0", val1_planes[0], list1)])]
        val2_mx = mx_tiles("vt2", N, "vt1_0_picked")
        weave_turned(SCALAR, woven_tile("vt2_a", 2, "vals2_%d" % LAST), turned2_low, val2_mx, 0)
        gr = weigh("gr_1a", 1, "gr_1a")
        weave_turned(SCALAR, woven_tile("vt2_b", 2, "vals1_0"), turned2_high, val2_mx, 2)
        gr_mx.append(mx_tiles("gr1", N))
        quantise_weights(1, gr)
        quantise_weights(2, weigh("gr_1b", 2, "vals1_0"))

        picked = pick_values("vt1_1", val1_planes[1], list1)
        woven = woven_tile("vt1_0", 1, "vals1_1")
        first_mx = mx_tiles("vt1_0", BLK)
        weave_turned(SCALAR, woven, turned1[0], first_mx, 0)
        turned1.append(turn([picked]))
        turned1.append(turn([pick_values("vt1_2", val1_planes[2], list1)]))
        picked = picked_tile("vt1_%d" % LAST)
        gather_split(picked[:], val1_planes[LAST], list1)
        turned1.append(turn([picked]))
        middle = held.tile([P, 2, N], BF16, name="middle_woven", tag="vals1_%d" % LAST, align_bytes=64)
        middle_mx = mx_tiles("vt1_middle", 2 * BLK)
        weave_turned(VECTOR, middle[:, 0], turned1[1], middle_mx, 0)
        weave_turned(SCALAR, middle[:, 1], turned1[2], middle_mx, 1)
        woven = woven_tile("vt1_3", 1, "vt1_3_woven")
        last_mx = mx_tiles("vt1_3", BLK)
        weave_turned(SCALAR, woven, turned1[LAST], last_mx, 0)
        val1 = [(first_mx, 0), (middle_mx, 0), (middle_mx, 1), (last_mx, 0)]

        result = held.tile([P, PACK, N], F32, name="result", tag="vt1_%d_picked" % LAST, align_bytes=64)
        for piece in range(2):
            for t in range(PACK):
                out_pass(t, piece, val2_mx, t, 1)
        for piece in range(2):
            out_pass(0, piece, *val1[0], 0)
        for t in range(PACK):
            out_pass(t, 2, val2_mx, t, 1)
        out_pass(0, 2, *val1[0], 0)
        for t in range(1, PACK):
            for piece in range(len(pieces)):
                out_pass(t, piece, *val1[t], 0)

        out_rows = out_0.rearrange("(p t) j -> p t j", t=PACK)
        for t, engine in enumerate((SCALAR, SCALAR, VECTOR)):
            copy(engine, result[:, t, :], out_banks[t][:].rearrange("p h j -> p (h j)"))
            nc.sync.dma_start(out_rows[:, t, :], result[:, t, :])

        woven_out = held.tile([P, N, PACK], BF16, name="woven_out", align_bytes=64)
        out_mx = mx_tiles("out", N)
        out_words = out_1[0].rearrange("p c r -> p (c r)").bitcast(I32)
        for h, cols in enumerate(halves):
            nc.scalar.copy(result[:, LAST, cols], last_banks[h][:])
        nc.sync.dma_start(out_rows[:, LAST, :], result[:, LAST, :])
        weave(VECTOR, woven_out, result, halves[0])
        weave(VECTOR, woven_out, result, slice(HALF, HALF + BLK))
        weave(SCALAR, woven_out, result, slice(HALF + BLK, N))
        for cols in halves:
            quantise(out_mx, cols, woven_out[:, cols, :].rearrange("p c t -> p (c t)"))
            nc.sync.dma_start(out_words[:, cols], out_mx[0][:, cols].bitcast(I32))
        for q in range(QUADRANTS):
            queue = nc.sync if q == QUADRANTS - 1 else nc.scalar
            queue.dma_start(
                out_2[0, 4 * q : 4 * q + 4, :].bitcast(I32), out_mx[1][32 * q : 32 * q + 4, :].bitcast(I32)
            )
